import numpy as np
import ml_dtypes


def mxq(x, axis, fmt="e4m3"):
    dtype, down = {"e4m3": (ml_dtypes.float8_e4m3fn, 7), "e5m2": (ml_dtypes.float8_e5m2, 14)}[fmt]
    v = np.moveaxis(np.asarray(x, np.float32).astype(ml_dtypes.bfloat16).astype(np.float64), axis, -1)
    blocks = v.reshape(v.shape[:-1] + (-1, 32))
    amax = np.abs(blocks).max(-1, keepdims=True)
    byte = np.maximum(np.where(amax > 0, np.frexp(amax)[1] - 1 + 127, 0) - down, 1)
    scale = np.exp2(byte - 127.0)
    codes = (blocks / scale).astype(np.float32).astype(dtype).astype(np.float64)
    return np.moveaxis((codes * scale).reshape(v.shape), -1, axis)


WIDE = False


def mx_kscale(k):
    if not WIDE:
        return np.ones(k)
    levels = np.array([10, -10, 5, -5, 0])
    if k % 512:
        return np.exp2(np.random.permutation(np.resize(levels, k // 32))).repeat(32)
    a = np.empty((k // 512, 16))
    for p in range(k // 512):
        a[p, :8] = np.random.permutation(np.resize(levels, 8))
        for g in range(8):
            far = levels[np.abs(levels - a[p, g]) >= 10]
            a[p, g + 8] = far[np.random.randint(len(far))]
    return np.exp2(a.ravel()).repeat(32)


def f64(x):
    return np.asarray(x).astype(np.float64)


def striped8(idx):
    return np.asarray(idx).reshape(8, -1, 16).transpose(0, 2, 1).reshape(128, -1).astype(np.uint16)


def unstriped8(offs):
    return offs.reshape(8, 16, -1).transpose(0, 2, 1).reshape(8, -1).astype(np.int64)


def pick8(x, idx, run):
    r = np.arange(len(x))
    return x[r[:, None], idx[r % (8 * run) // run]]


E2M1 = np.array([0.0, 0.5, 1.0, 1.5, 2.0, 3.0, 4.0, 6.0, -0.0, -0.5, -1.0, -1.5, -2.0, -3.0, -4.0, -6.0])


def pack_weight(w, fmt):
    k, n = w.shape
    w = f64(np.asarray(w, np.float32).astype(ml_dtypes.bfloat16)).reshape(k // 32, 32, n)
    amax = np.abs(w).max(1)
    if fmt == "e4m3":
        byte = np.frexp(amax)[1] - 1 + 127 - 7
    else:
        mant, ex = np.frexp(amax / 6.0)
        byte = np.where(mant > 0.5, ex, ex - 1) + 127
    byte = np.clip(np.where(amax > 0, byte, 1), 1, 254)
    scaled = (w * np.exp2(127.0 - byte)[:, None, :]).reshape(k, n).astype(np.float32)
    by_word = np.ascontiguousarray(scaled.reshape(k // 512, 128, 4, n).transpose(0, 1, 3, 2))
    if fmt == "e4m3":
        words = by_word.astype(ml_dtypes.float8_e4m3fn).view(np.uint8)
    else:
        c = by_word.astype(ml_dtypes.float4_e2m1fn).view(np.uint8) & 0xF
        words = (c[..., 0::2] | (c[..., 1::2] << 4)).reshape(k // 512, 128, 2 * n)
    return np.ascontiguousarray(words), np.ascontiguousarray(byte.astype(np.uint8).reshape(k // 512, 16, n))


def unpack_weight(words, scales, fmt):
    g, _, n = scales.shape
    words = np.ascontiguousarray(words).reshape(g, 128, n, -1)
    if fmt == "e4m3":
        vals = words.view(ml_dtypes.float8_e4m3fn).astype(np.float64)
    else:
        nib = np.empty((g, 128, n, 4), np.uint8)
        nib[..., 0::2] = words & 0xF
        nib[..., 1::2] = words >> 4
        vals = E2M1[nib]
    vals = vals * np.repeat(np.exp2(scales.astype(np.float64) - 127.0), 8, axis=1)[..., None]
    return vals.transpose(0, 1, 3, 2).reshape(g * 512, n)


D, T, U, Z, I, Q, E = 512, 1024, 1024, 1024, 512, 512, 256


def setup_inputs():
    n = np.random.standard_normal
    idx = np.stack([np.random.permutation(T)[:I] for _ in range(8)])
    idx2 = np.stack([np.random.permutation(U)[:I] for _ in range(8)])
    idx3 = np.stack([np.random.permutation(Z)[:I] for _ in range(8)])
    idx4 = np.stack([np.random.permutation(Z)[:I] for _ in range(8)])
    idx5 = np.stack([np.random.permutation(Z)[:I] for _ in range(8)])
    fd = mx_kscale(D)
    fq = mx_kscale(Q)
    cachep = pack_weight(n((D, T)) / fd[:, None], "e4m3")
    draftp = pack_weight(n((D, U)) / fd[:, None], "e2m1")
    mixp = pack_weight(n((Q, E)) * 1.0 / np.sqrt(Q) / fq[:, None], "e2m1")
    return {
        "query": (n((D, Q)) * 1.0 / np.sqrt(D) * fd[:, None]).astype(np.float32),
        "cache_words": cachep[0],
        "cache_scales": cachep[1],
        "draft_words": draftp[0],
        "draft_scales": draftp[1],
        "rowf": (np.random.uniform(0.5, 2.0, (Q, 1)) * fq[:, None]).astype(np.float32),
        "mix_words": mixp[0],
        "mix_scales": mixp[1],
        "offs": striped8(idx),
        "offs2": striped8(idx2),
        "offs3": striped8(idx3),
        "offs4": striped8(idx4),
        "offs5": striped8(idx5),
    }


def reference(query, cache_words, cache_scales, draft_words, draft_scales, rowf, mix_words, mix_scales, offs, offs2, offs3, offs4, offs5):
    idx = unstriped8(offs)
    idx2 = unstriped8(offs2)
    idx3 = unstriped8(offs3)
    idx4 = unstriped8(offs4)
    idx5 = unstriped8(offs5)
    cacheu = unpack_weight(cache_words, cache_scales, "e4m3")
    draftu = unpack_weight(draft_words, draft_scales, "e2m1")
    mixu = unpack_weight(mix_words, mix_scales, "e2m1")
    queryq = mxq(f64(query), 0, "e4m3")
    a = queryq.T @ cacheu
    b = queryq.T @ draftu
    g = np.minimum(pick8(a, idx, 64), pick8(b, idx2, 64))
    gw = g * f64(rowf)
    gwq = mxq(gw, 0, "e4m3")
    o1 = mixu.T @ gwq
    pa = np.zeros((E, Z))
    pa[np.arange(E)[:, None], idx3[np.arange(E) % 128 // 16]] = o1
    pb = np.zeros((E, Z))
    pb[np.arange(E)[:, None], idx4[np.arange(E) % 128 // 16]] = o1
    m1 = np.minimum(pa, pb)
    y = pick8(m1, idx5, 16) + o1
    return y

@@ -1,0 +1,216 @@
+from contextlib import ExitStack
+
+import concourse.mybir as mybir
+
+D, T, Z, I, Q, E = 512, 1024, 1024, 512, 512, 256
+FLOPS = 2 * D * Q * 2 * T + 2 * Q * E * I
+
+F32 = mybir.dt.float32
+BF16 = mybir.dt.bfloat16
+I32 = mybir.dt.int32
+U16 = mybir.dt.uint16
+U8 = mybir.dt.uint8
+FP8X4 = mybir.dt.float8_e4m3fn_x4
+FP4X4 = mybir.dt.float4_e2m1fn_x4
+COPY = mybir.ActivationFunctionType.Copy
+MIN = mybir.AluOpType.min
+MULT = mybir.AluOpType.mult
+ADD = mybir.AluOpType.add
+
+P = 128
+PACK = 4
+BANK = 512
+HALF = 256
+M_VECTOR = 44
+
+
+def tile_attend_lowertwo_two_postkept_kernel(
+    tc, query, cache_words, cache_scales, draft_words, draft_scales, rowf, mix_words, mix_scales,
+    offs, offs2, offs3, offs4, offs5, out,
+):
+    nc = tc.nc
+    with ExitStack() as ctx:
+        keep = ctx.enter_context(tc.tile_pool(name="keep", bufs=1))
+        score_psum = ctx.enter_context(tc.psum_pool(name="score_psum", bufs=6))
+        mix_psum = ctx.enter_context(tc.psum_pool(name="mix_psum", bufs=2))
+
+        def sb(name, shape, dtype, tag=""):
+            return keep.tile(shape, dtype, name=name, tag=tag or name, align_bytes=64)
+
+        def load_plane(plane, scales):
+            for quad in range(4):
+                nc.sync.dma_start(
+                    out=plane[32 * quad : 32 * quad + 4, :].bitcast(I32),
+                    in_=scales[0, 4 * quad : 4 * quad + 4, :].bitcast(I32),
+                )
+
+        cache_plane = sb("cache_plane", [P, T], U8)
+        draft_plane = sb("draft_plane", [P, T], U8)
+        mix_plane = sb("mix_plane", [P, E], U8)
+        for plane in (cache_plane, draft_plane, mix_plane):
+            nc.vector.memset(plane[:].bitcast(I32), 0)
+
+        query_rows = query.rearrange("(p j) q -> p j q", j=PACK)
+        raw = [sb(f"raw{c}", [P, PACK, Q // 2], F32) for c in range(2)]
+        for c in range(2):
+            nc.sync.dma_start(out=raw[c][:], in_=query_rows[:, :, c * (Q // 2) : (c + 1) * (Q // 2)])
+        load_plane(cache_plane, cache_scales)
+        cache_rows = cache_words[0].rearrange("p n t -> p (n t)").bitcast(I32)
+        cache_codes = [sb(f"cache_codes{h}", [P, BANK], I32) for h in range(2)]
+        for h in range(2):
+            nc.sync.dma_start(out=cache_codes[h][:], in_=cache_rows[:, h * BANK : (h + 1) * BANK])
+        load_plane(draft_plane, draft_scales)
+        draft_codes = sb("draft_codes", [P, 2 * T], U8)
+        nc.sync.dma_start(out=draft_codes[:].bitcast(I32), in_=draft_words[0].bitcast(I32))
+        lists = {}
+        for name, src in (("offs", offs), ("offs2", offs2)):
+            lists[name] = sb(name, [P, I // 16], U16)
+            nc.sync.dma_start(lists[name][:], src)
+        row_factor = sb("row_factor", [P, PACK], F32)
+        nc.sync.dma_start(out=row_factor[:], in_=rowf.rearrange("(p t) o -> p (t o)", t=PACK))
+        mix_codes = sb("mix_codes", [P, 2 * E], U8)
+        nc.sync.dma_start(out=mix_codes[:].bitcast(I32), in_=mix_words[0].bitcast(I32))
+        load_plane(mix_plane, mix_scales)
+        for name, src in (("offs3", offs3), ("offs4", offs4), ("offs5", offs5)):
+            lists[name] = sb(name, [P, I // 16], U16)
+            nc.sync.dma_start(lists[name][:], src)
+
+        def listed(window, name, first, count):
+            return window[:].indirect(lists[name][:, first // 16 : (first + count) // 16])
+
+        pages = [[sb(f"page{et}{k}", [P, Z], F32) for k in range(2)] for et in range(2)]
+        for et in range(2):
+            for k in range(2):
+                nc.vector.memset(pages[et][k][:], 0.0)
+
+        q_bf = sb("q_bf", [P, PACK, P, PACK], BF16)
+        for c in range(2):
+            src = raw[c][:].rearrange("p j (m t) -> p m t j", t=PACK)
+            dst = q_bf[:, :, 64 * c : 64 * (c + 1), :].rearrange("p t m j -> p m t j")
+            nc.scalar.copy(out=dst[:, M_VECTOR:], in_=src[:, M_VECTOR:])
+            nc.vector.tensor_copy(out=dst[:, :M_VECTOR], in_=src[:, :M_VECTOR])
+        q_codes = [sb(f"q_codes{t}", [P, P], I32) for t in range(PACK)]
+        q_plane = [sb(f"q_plane{t}", [P, P], U8) for t in range(PACK)]
+        for t in range(PACK):
+            nc.vector.quantize_mx(
+                out=q_codes[t][:].bitcast(FP8X4), scales=q_plane[t][:],
+                in_=q_bf[:, t].rearrange("p m j -> p (m j)"),
+            )
+
+        windows = {name: [sb(f"{name}{t}", [P, T], F32) for t in range(PACK)] for name in ("a", "b")}
+        low = sb("low", [P, PACK, HALF], F32)
+        other = sb("other", [P, PACK, HALF], F32)
+
+        def scores(name, t, second_on_vector):
+            for h in range(2):
+                cols = slice(h * BANK, (h + 1) * BANK)
+                bank = score_psum.tile([P, BANK], F32, name="bank")
+                if name == "a":
+                    rhs, rhs_scale = cache_codes[h][:].bitcast(FP8X4), cache_plane[:, cols]
+                else:
+                    rhs, rhs_scale = draft_codes[:, 2 * h * BANK : 2 * (h + 1) * BANK].bitcast(FP4X4), draft_plane[:, cols]
+                nc.tensor.matmul_mx(
+                    out=bank[:], lhsT=q_codes[t][:].bitcast(FP8X4), lhsT_scale=q_plane[t][:],
+                    rhs=rhs, rhs_scale=rhs_scale, start=True, stop=True,
+                )
+                if h == 0 or not second_on_vector:
+                    nc.scalar.copy(out=windows[name][t][:, cols], in_=bank[:])
+                else:
+                    nc.vector.tensor_copy(out=windows[name][t][:, cols], in_=bank[:])
+
+        def gather(dst, name, t, h, on_scalar):
+            src = listed(windows[name][t], "offs" if name == "a" else "offs2", h * HALF, HALF)
+            if on_scalar:
+                nc.scalar.activation(dst, src, COPY)
+            else:
+                nc.vector.tensor_copy(dst, src)
+
+        def take_lower(x, y):
+            nc.vector.tensor_tensor(x, x, y, MIN)
+
+        o1 = sb("o1", [P, 2, I], F32)
+
+        def mix(first, count, on_scalar):
+            lo = first % HALF
+            gw = sb(f"gw{first}", [P, count, PACK], BF16)
+            nc.vector.tensor_tensor(
+                gw[:], low[:, :, lo : lo + count].rearrange("p t i -> p i t"),
+                row_factor[:].rearrange("p (o t) -> p o t", o=1).to_broadcast([P, count, PACK]), MULT,
+            )
+            codes = sb(f"gw_codes{first}", [P, count], I32)
+            plane = sb(f"gw_plane{first}", [P, count], U8)
+            nc.vector.quantize_mx(out=codes[:].bitcast(FP8X4), scales=plane[:], in_=gw[:].rearrange("p i t -> p (i t)"))
+            bank = mix_psum.tile([P, 2, count], F32, name="mix_bank")
+            for et in range(2):
+                nc.tensor.matmul_mx(
+                    out=bank[:, et, :], lhsT=mix_codes[:, 2 * P * et : 2 * P * (et + 1)].bitcast(FP4X4),
+                    lhsT_scale=mix_plane[:, P * et : P * (et + 1)],
+                    rhs=codes[:].bitcast(FP8X4), rhs_scale=plane[:], start=True, stop=True,
+                )
+            if on_scalar:
+                nc.scalar.copy(out=o1[:, :, first : first + count], in_=bank[:])
+            else:
+                nc.vector.tensor_copy(out=o1[:, :, first : first + count], in_=bank[:])
+
+        def scatter(et, first, count):
+            for k, name in enumerate(("offs3", "offs4")):
+                nc.scalar.activation(listed(pages[et][k], name, first, count), o1[:, et, first : first + count], COPY)
+
+        def lower_page(et):
+            m1 = sb(f"m1_{et}", [P, Z], F32)
+            nc.vector.tensor_tensor(m1[:], pages[et][0][:], pages[et][1][:], MIN)
+            return m1
+
+        scores("a", 0, True)
+        gather(low[:, 0, :], "a", 0, 0, False)
+        scores("a", 1, True)
+        gather(low[:, 1, :], "a", 1, 0, False)
+        scores("b", 0, False)
+        gather(other[:, 0, :], "b", 0, 0, False)
+        take_lower(low[:, 0, :], other[:, 0, :])
+        scores("b", 1, False)
+        gather(other[:, 1, :], "b", 1, 0, False)
+        take_lower(low[:, 1, :], other[:, 1, :])
+        scores("a", 2, False)
+        gather(low[:, 2, :], "a", 2, 0, False)
+        scores("b", 2, False)
+        scores("a", 3, True)
+        gather(other[:, 2, :], "b", 2, 0, False)
+        scores("b", 3, True)
+        gather(low[:, 3, :], "a", 3, 0, True)
+        gather(other[:, 3, :], "b", 3, 0, False)
+        take_lower(low[:, 2:, :128], other[:, 2:, :128])
+        late = [sb(f"late{h}", [P, 2, HALF], F32, tag=f"cache_codes{h}") for h in range(2)]
+        late_a = [late[0][:, 0, :], late[0][:, 1, :], late[1][:, 0, :]]
+        for t in range(3):
+            gather(late_a[t], "a", t, 1, True)
+        mix(0, 128, True)
+        for et in range(2):
+            scatter(et, 0, 128)
+        take_lower(low[:, 2:, 128:], other[:, 2:, 128:])
+        mix(128, 128, False)
+        for et in range(2):
+            scatter(et, 128, 128)
+        late3 = sb("late3", [P, HALF], F32, tag="gw0")
+        late_a.append(late3[:])
+        gather(late_a[3], "a", 3, 1, False)
+        for t in range(PACK):
+            gather(low[:, t, :], "b", t, 1, False)
+            take_lower(low[:, t, :], late_a[t])
+        mix(256, 128, False)
+        mix(384, 128, False)
+        scatter(0, 256, 128)
+        scatter(0, 384, 128)
+        m1 = lower_page(0)
+        y0 = sb("y0", [P, I], F32)
+        nc.vector.tensor_tensor(y0[:], listed(m1, "offs5", 0, I), o1[:, 0, :], ADD)
+        nc.sync.dma_start(out=out[:P, :], in_=y0[:])
+        scatter(1, 256, 256)
+        m1 = lower_page(1)
+        y1 = [sb(f"y1{h}", [P, HALF], F32) for h in range(2)]
+        kept = sb("kept", [P, HALF], F32)
+        nc.scalar.activation(kept[:], listed(m1, "offs5", HALF, HALF), COPY)
+        nc.vector.tensor_tensor(y1[0][:], listed(m1, "offs5", 0, HALF), o1[:, 1, :HALF], ADD)
+        nc.sync.dma_start(out=out[P:, :HALF], in_=y1[0][:])
+        nc.vector.tensor_tensor(y1[1][:], kept[:], o1[:, 1, HALF:], ADD)
+        nc.sync.dma_start(out=out[P:, HALF:], in_=y1[1][:])

@@ -21,7 +21,7 @@ P = 128
 PACK = 4
 BANK = 512
 HALF = 256
-M_VECTOR = 44
+QUERY_PIECES = ((0, 80, 54), (80, 48, 32))
 
 
 def tile_attend_lowertwo_two_postkept_kernel(
@@ -31,8 +31,7 @@ def tile_attend_lowertwo_two_postkept_kernel(
     nc = tc.nc
     with ExitStack() as ctx:
         keep = ctx.enter_context(tc.tile_pool(name="keep", bufs=1))
-        score_psum = ctx.enter_context(tc.psum_pool(name="score_psum", bufs=6))
-        mix_psum = ctx.enter_context(tc.psum_pool(name="mix_psum", bufs=2))
+        psum = ctx.enter_context(tc.psum_pool(name="psum", bufs=8))
 
         def sb(name, shape, dtype, tag=""):
             return keep.tile(shape, dtype, name=name, tag=tag or name, align_bytes=64)
@@ -51,14 +50,14 @@ def tile_attend_lowertwo_two_postkept_kernel(
             nc.vector.memset(plane[:].bitcast(I32), 0)
 
         query_rows = query.rearrange("(p j) q -> p j q", j=PACK)
-        raw = [sb(f"raw{c}", [P, PACK, Q // 2], F32) for c in range(2)]
-        for c in range(2):
-            nc.sync.dma_start(out=raw[c][:], in_=query_rows[:, :, c * (Q // 2) : (c + 1) * (Q // 2)])
+        raw = [sb(f"raw{m0}", [P, PACK, PACK * ms], F32) for m0, ms, share in QUERY_PIECES]
+        for c, (m0, ms, share) in enumerate(QUERY_PIECES):
+            nc.sync.dma_start(out=raw[c][:], in_=query_rows[:, :, PACK * m0 : PACK * (m0 + ms)])
         load_plane(cache_plane, cache_scales)
         cache_rows = cache_words[0].rearrange("p n t -> p (n t)").bitcast(I32)
-        cache_codes = [sb(f"cache_codes{h}", [P, BANK], I32) for h in range(2)]
+        cache_codes = sb("cache_codes", [P, T], I32)
         for h in range(2):
-            nc.sync.dma_start(out=cache_codes[h][:], in_=cache_rows[:, h * BANK : (h + 1) * BANK])
+            nc.sync.dma_start(out=cache_codes[:, h * BANK : (h + 1) * BANK], in_=cache_rows[:, h * BANK : (h + 1) * BANK])
         load_plane(draft_plane, draft_scales)
         draft_codes = sb("draft_codes", [P, 2 * T], U8)
         nc.sync.dma_start(out=draft_codes[:].bitcast(I32), in_=draft_words[0].bitcast(I32))
@@ -81,14 +80,14 @@ def tile_attend_lowertwo_two_postkept_kernel(
         pages = [[sb(f"page{et}{k}", [P, Z], F32) for k in range(2)] for et in range(2)]
         for et in range(2):
             for k in range(2):
-                nc.vector.memset(pages[et][k][:], 0.0)
+                nc.vector.memset(pages[et][k][:].bitcast(I32), 0)
 
         q_bf = sb("q_bf", [P, PACK, P, PACK], BF16)
-        for c in range(2):
+        for c, (m0, ms, share) in enumerate(QUERY_PIECES):
             src = raw[c][:].rearrange("p j (m t) -> p m t j", t=PACK)
-            dst = q_bf[:, :, 64 * c : 64 * (c + 1), :].rearrange("p t m j -> p m t j")
-            nc.scalar.copy(out=dst[:, M_VECTOR:], in_=src[:, M_VECTOR:])
-            nc.vector.tensor_copy(out=dst[:, :M_VECTOR], in_=src[:, :M_VECTOR])
+            dst = q_bf[:, :, m0 : m0 + ms, :].rearrange("p t m j -> p m t j")
+            nc.scalar.copy(out=dst[:, share:], in_=src[:, share:])
+            nc.vector.tensor_copy(out=dst[:, :share], in_=src[:, :share])
         q_codes = [sb(f"q_codes{t}", [P, P], I32) for t in range(PACK)]
         q_plane = [sb(f"q_plane{t}", [P, P], U8) for t in range(PACK)]
         for t in range(PACK):
@@ -99,21 +98,20 @@ def tile_attend_lowertwo_two_postkept_kernel(
 
         windows = {name: [sb(f"{name}{t}", [P, T], F32) for t in range(PACK)] for name in ("a", "b")}
         low = sb("low", [P, PACK, HALF], F32)
-        other = sb("other", [P, PACK, HALF], F32)
 
-        def scores(name, t, second_on_vector):
+        def scores(name, t):
             for h in range(2):
                 cols = slice(h * BANK, (h + 1) * BANK)
-                bank = score_psum.tile([P, BANK], F32, name="bank")
+                bank = psum.tile([P, BANK], F32, name="bank")
                 if name == "a":
-                    rhs, rhs_scale = cache_codes[h][:].bitcast(FP8X4), cache_plane[:, cols]
+                    rhs, rhs_scale = cache_codes[:, cols].bitcast(FP8X4), cache_plane[:, cols]
                 else:
                     rhs, rhs_scale = draft_codes[:, 2 * h * BANK : 2 * (h + 1) * BANK].bitcast(FP4X4), draft_plane[:, cols]
                 nc.tensor.matmul_mx(
                     out=bank[:], lhsT=q_codes[t][:].bitcast(FP8X4), lhsT_scale=q_plane[t][:],
                     rhs=rhs, rhs_scale=rhs_scale, start=True, stop=True,
                 )
-                if h == 0 or not second_on_vector:
+                if h == 0:
                     nc.scalar.copy(out=windows[name][t][:, cols], in_=bank[:])
                 else:
                     nc.vector.tensor_copy(out=windows[name][t][:, cols], in_=bank[:])
@@ -125,32 +123,34 @@ def tile_attend_lowertwo_two_postkept_kernel(
             else:
                 nc.vector.tensor_copy(dst, src)
 
-        def take_lower(x, y):
-            nc.vector.tensor_tensor(x, x, y, MIN)
+        def take_lower(x, y, dst=None):
+            nc.vector.tensor_tensor(x if dst is None else dst, x, y, MIN)
 
         o1 = sb("o1", [P, 2, I], F32)
 
-        def mix(first, count, on_scalar):
-            lo = first % HALF
-            gw = sb(f"gw{first}", [P, count, PACK], BF16)
-            nc.vector.tensor_tensor(
-                gw[:], low[:, :, lo : lo + count].rearrange("p t i -> p i t"),
-                row_factor[:].rearrange("p (o t) -> p o t", o=1).to_broadcast([P, count, PACK]), MULT,
+        def weigh(rounded, g, ts):
+            for t in ts:
+                nc.vector.tensor_scalar(rounded[:, t, :], g[:, t, :], row_factor[:, t : t + 1], None, MULT)
+
+        def mix(rounded, first, apart, tag=""):
+            gw = sb(f"gw{first}", [P, 128, PACK], BF16, tag=tag)
+            nc.vector.tensor_copy(
+                out=gw[:].rearrange("p (c i) t -> p c t i", i=4), in_=rounded[:].rearrange("p t (c i) -> p c t i", i=4)
             )
-            codes = sb(f"gw_codes{first}", [P, count], I32)
-            plane = sb(f"gw_plane{first}", [P, count], U8)
+            codes = sb(f"gw_codes{first}", [P, 128], I32)
+            plane = sb(f"gw_plane{first}", [P, 128], U8)
             nc.vector.quantize_mx(out=codes[:].bitcast(FP8X4), scales=plane[:], in_=gw[:].rearrange("p i t -> p (i t)"))
-            bank = mix_psum.tile([P, 2, count], F32, name="mix_bank")
             for et in range(2):
+                bank = psum.tile([P, BANK], F32, name="bank")
                 nc.tensor.matmul_mx(
-                    out=bank[:, et, :], lhsT=mix_codes[:, 2 * P * et : 2 * P * (et + 1)].bitcast(FP4X4),
+                    out=bank[:, :128], lhsT=mix_codes[:, 2 * P * et : 2 * P * (et + 1)].bitcast(FP4X4),
                     lhsT_scale=mix_plane[:, P * et : P * (et + 1)],
                     rhs=codes[:].bitcast(FP8X4), rhs_scale=plane[:], start=True, stop=True,
                 )
-            if on_scalar:
-                nc.scalar.copy(out=o1[:, :, first : first + count], in_=bank[:])
-            else:
-                nc.vector.tensor_copy(out=o1[:, :, first : first + count], in_=bank[:])
+                if apart:
+                    nc.scalar.copy(out=o1[:, et, first : first + 128], in_=bank[:, :128])
+                else:
+                    nc.vector.tensor_copy(out=o1[:, et, first : first + 128], in_=bank[:, :128])
 
         def scatter(et, first, count):
             for k, name in enumerate(("offs3", "offs4")):
@@ -161,44 +161,47 @@ def tile_attend_lowertwo_two_postkept_kernel(
             nc.vector.tensor_tensor(m1[:], pages[et][0][:], pages[et][1][:], MIN)
             return m1
 
-        scores("a", 0, True)
+        rounded = [sb(f"rounded{c}", [P, PACK, 128], BF16) for c in range(3)]
+        scores("a", 0)
         gather(low[:, 0, :], "a", 0, 0, False)
-        scores("a", 1, True)
-        gather(low[:, 1, :], "a", 1, 0, False)
-        scores("b", 0, False)
+        for name, t in (("a", 1), ("b", 0), ("b", 1), ("a", 2), ("b", 2), ("a", 3), ("b", 3)):
+            scores(name, t)
+        other = sb("other", [P, PACK, HALF], F32, tag="cache_codes")
+        gather(low[:, 1, :], "a", 1, 0, True)
         gather(other[:, 0, :], "b", 0, 0, False)
-        take_lower(low[:, 0, :], other[:, 0, :])
-        scores("b", 1, False)
-        gather(other[:, 1, :], "b", 1, 0, False)
-        take_lower(low[:, 1, :], other[:, 1, :])
-        scores("a", 2, False)
-        gather(low[:, 2, :], "a", 2, 0, False)
-        scores("b", 2, False)
-        scores("a", 3, True)
+        gather(other[:, 1, :], "b", 1, 0, True)
         gather(other[:, 2, :], "b", 2, 0, False)
-        scores("b", 3, True)
-        gather(low[:, 3, :], "a", 3, 0, True)
+        gather(low[:, 2, :], "a", 2, 0, True)
         gather(other[:, 3, :], "b", 3, 0, False)
+        gather(low[:, 3, :], "a", 3, 0, True)
+        take_lower(low[:, :2, :128], other[:, :2, :128])
         take_lower(low[:, 2:, :128], other[:, 2:, :128])
-        late = [sb(f"late{h}", [P, 2, HALF], F32, tag=f"cache_codes{h}") for h in range(2)]
-        late_a = [late[0][:, 0, :], late[0][:, 1, :], late[1][:, 0, :]]
-        for t in range(3):
-            gather(late_a[t], "a", t, 1, True)
-        mix(0, 128, True)
+        weigh(rounded[0], low[:, :, :128], range(PACK))
+        late = sb("late", [P, PACK, HALF], F32, tag="draft_codes")
+        for t in range(PACK):
+            gather(late[:, t, :], "a", t, 1, True)
+        mix(rounded[0], 0, True)
         for et in range(2):
             scatter(et, 0, 128)
-        take_lower(low[:, 2:, 128:], other[:, 2:, 128:])
-        mix(128, 128, False)
+        g1 = sb("g1", [P, PACK, 128], F32, tag="gw0")
+        take_lower(low[:, :, 128:], other[:, :, 128:], g1[:])
+        weigh(rounded[1], g1[:], range(PACK))
+        mix(rounded[1], 128, False)
         for et in range(2):
             scatter(et, 128, 128)
-        late3 = sb("late3", [P, HALF], F32, tag="gw0")
-        late_a.append(late3[:])
-        gather(late_a[3], "a", 3, 1, False)
-        for t in range(PACK):
-            gather(low[:, t, :], "b", t, 1, False)
-            take_lower(low[:, t, :], late_a[t])
-        mix(256, 128, False)
-        mix(384, 128, False)
+        third = sb("third", [P, HALF], F32, tag="gw128")
+        fourth = sb("fourth", [P, HALF], F32, tag="gw_codes128")
+        for t, dst in enumerate((low[:, 0, :], low[:, 1, :], third[:], fourth[:])):
+            gather(dst, "b", t, 1, False)
+        for c in (2, 3):
+            cols = slice(128 * (c - 2), 128 * (c - 1))
+            take_lower(late[:, :2, cols], low[:, :2, cols])
+            take_lower(late[:, 2, cols], third[:, cols])
+            take_lower(late[:, 3, cols], fourth[:, cols])
+            if c == 3:
+                rounded.append(sb("rounded3", [P, PACK, 128], BF16, tag="gw256"))
+            weigh(rounded[c], late[:, :, cols], range(PACK))
+            mix(rounded[c], 128 * c, False)
         scatter(0, 256, 128)
         scatter(0, 384, 128)
         m1 = lower_page(0)

@@ -21,7 +21,7 @@ P = 128
 PACK = 4
 BANK = 512
 HALF = 256
-QUERY_PIECES = ((0, 80, 54), (80, 48, 32))
+QUERY_PIECES = ((0, 64, 44), (64, 64, 44))
 
 
 def tile_attend_lowertwo_two_postkept_kernel(
@@ -128,14 +128,11 @@ def tile_attend_lowertwo_two_postkept_kernel(
 
         o1 = sb("o1", [P, 2, I], F32)
 
-        def weigh(rounded, g, ts):
-            for t in ts:
-                nc.vector.tensor_scalar(rounded[:, t, :], g[:, t, :], row_factor[:, t : t + 1], None, MULT)
-
-        def mix(rounded, first, apart, tag=""):
+        def mix(g, first, apart, tag=""):
             gw = sb(f"gw{first}", [P, 128, PACK], BF16, tag=tag)
-            nc.vector.tensor_copy(
-                out=gw[:].rearrange("p (c i) t -> p c t i", i=4), in_=rounded[:].rearrange("p t (c i) -> p c t i", i=4)
+            nc.vector.tensor_tensor(
+                gw[:], g.rearrange("p t i -> p i t"),
+                row_factor[:].rearrange("p (o t) -> p o t", o=1).to_broadcast([P, 128, PACK]), MULT,
             )
             codes = sb(f"gw_codes{first}", [P, 128], I32)
             plane = sb(f"gw_plane{first}", [P, 128], U8)
@@ -157,11 +154,10 @@ def tile_attend_lowertwo_two_postkept_kernel(
                 nc.scalar.activation(listed(pages[et][k], name, first, count), o1[:, et, first : first + count], COPY)
 
         def lower_page(et):
-            m1 = sb(f"m1_{et}", [P, Z], F32)
+            m1 = sb(f"m1_{et}", [P, Z], F32, tag="m1")
             nc.vector.tensor_tensor(m1[:], pages[et][0][:], pages[et][1][:], MIN)
             return m1
 
-        rounded = [sb(f"rounded{c}", [P, PACK, 128], BF16) for c in range(3)]
         scores("a", 0)
         gather(low[:, 0, :], "a", 0, 0, False)
         for name, t in (("a", 1), ("b", 0), ("b", 1), ("a", 2), ("b", 2), ("a", 3), ("b", 3)):
@@ -176,17 +172,15 @@ def tile_attend_lowertwo_two_postkept_kernel(
         gather(low[:, 3, :], "a", 3, 0, True)
         take_lower(low[:, :2, :128], other[:, :2, :128])
         take_lower(low[:, 2:, :128], other[:, 2:, :128])
-        weigh(rounded[0], low[:, :, :128], range(PACK))
         late = sb("late", [P, PACK, HALF], F32, tag="draft_codes")
         for t in range(PACK):
             gather(late[:, t, :], "a", t, 1, True)
-        mix(rounded[0], 0, True)
+        mix(low[:, :, :128], 0, True)
         for et in range(2):
             scatter(et, 0, 128)
         g1 = sb("g1", [P, PACK, 128], F32, tag="gw0")
         take_lower(low[:, :, 128:], other[:, :, 128:], g1[:])
-        weigh(rounded[1], g1[:], range(PACK))
-        mix(rounded[1], 128, False)
+        mix(g1[:], 128, False)
         for et in range(2):
             scatter(et, 128, 128)
         third = sb("third", [P, HALF], F32, tag="gw128")
@@ -198,10 +192,7 @@ def tile_attend_lowertwo_two_postkept_kernel(
             take_lower(late[:, :2, cols], low[:, :2, cols])
             take_lower(late[:, 2, cols], third[:, cols])
             take_lower(late[:, 3, cols], fourth[:, cols])
-            if c == 3:
-                rounded.append(sb("rounded3", [P, PACK, 128], BF16, tag="gw256"))
-            weigh(rounded[c], late[:, :, cols], range(PACK))
-            mix(rounded[c], 128 * c, False)
+            mix(late[:, :, cols], 128 * c, False, tag="gw256" if c == 3 else "")
         scatter(0, 256, 128)
         scatter(0, 384, 128)
         m1 = lower_page(0)

@@ -128,11 +128,14 @@ def tile_attend_lowertwo_two_postkept_kernel(
 
         o1 = sb("o1", [P, 2, I], F32)
 
-        def mix(g, first, apart, tag=""):
+        def weigh(rounded, g, ts):
+            for t in ts:
+                nc.vector.tensor_scalar(rounded[:, t, :], g[:, t, :], row_factor[:, t : t + 1], None, MULT)
+
+        def mix(rounded, first, apart, tag=""):
             gw = sb(f"gw{first}", [P, 128, PACK], BF16, tag=tag)
-            nc.vector.tensor_tensor(
-                gw[:], g.rearrange("p t i -> p i t"),
-                row_factor[:].rearrange("p (o t) -> p o t", o=1).to_broadcast([P, 128, PACK]), MULT,
+            nc.vector.tensor_copy(
+                out=gw[:].rearrange("p (c i) t -> p c t i", i=4), in_=rounded[:].rearrange("p t (c i) -> p c t i", i=4)
             )
             codes = sb(f"gw_codes{first}", [P, 128], I32)
             plane = sb(f"gw_plane{first}", [P, 128], U8)
@@ -158,6 +161,7 @@ def tile_attend_lowertwo_two_postkept_kernel(
             nc.vector.tensor_tensor(m1[:], pages[et][0][:], pages[et][1][:], MIN)
             return m1
 
+        rounded = [sb(f"rounded{c}", [P, PACK, 128], BF16) for c in range(3)]
         scores("a", 0)
         gather(low[:, 0, :], "a", 0, 0, False)
         for name, t in (("a", 1), ("b", 0), ("b", 1), ("a", 2), ("b", 2), ("a", 3), ("b", 3)):
@@ -172,15 +176,17 @@ def tile_attend_lowertwo_two_postkept_kernel(
         gather(low[:, 3, :], "a", 3, 0, True)
         take_lower(low[:, :2, :128], other[:, :2, :128])
         take_lower(low[:, 2:, :128], other[:, 2:, :128])
+        weigh(rounded[0], low[:, :, :128], range(PACK))
         late = sb("late", [P, PACK, HALF], F32, tag="draft_codes")
         for t in range(PACK):
             gather(late[:, t, :], "a", t, 1, True)
-        mix(low[:, :, :128], 0, True)
+        mix(rounded[0], 0, True)
         for et in range(2):
             scatter(et, 0, 128)
         g1 = sb("g1", [P, PACK, 128], F32, tag="gw0")
         take_lower(low[:, :, 128:], other[:, :, 128:], g1[:])
-        mix(g1[:], 128, False)
+        weigh(rounded[1], g1[:], range(PACK))
+        mix(rounded[1], 128, False)
         for et in range(2):
             scatter(et, 128, 128)
         third = sb("third", [P, HALF], F32, tag="gw128")
@@ -192,7 +198,10 @@ def tile_attend_lowertwo_two_postkept_kernel(
             take_lower(late[:, :2, cols], low[:, :2, cols])
             take_lower(late[:, 2, cols], third[:, cols])
             take_lower(late[:, 3, cols], fourth[:, cols])
-            mix(late[:, :, cols], 128 * c, False, tag="gw256" if c == 3 else "")
+            if c == 3:
+                rounded.append(sb("rounded3", [P, PACK, 128], BF16, tag="gw256"))
+            weigh(rounded[c], late[:, :, cols], range(PACK))
+            mix(rounded[c], 128 * c, False)
         scatter(0, 256, 128)
         scatter(0, 384, 128)
         m1 = lower_page(0)

from contextlib import ExitStack

import concourse.mybir as mybir

D, T, Z, I, Q, E = 512, 1024, 1024, 512, 512, 256
FLOPS = 2 * D * Q * 2 * T + 2 * Q * E * I

F32 = mybir.dt.float32
BF16 = mybir.dt.bfloat16
I32 = mybir.dt.int32
U16 = mybir.dt.uint16
U8 = mybir.dt.uint8
FP8X4 = mybir.dt.float8_e4m3fn_x4
FP4X4 = mybir.dt.float4_e2m1fn_x4
COPY = mybir.ActivationFunctionType.Copy
MIN = mybir.AluOpType.min
MULT = mybir.AluOpType.mult
ADD = mybir.AluOpType.add

P = 128
PACK = 4
BANK = 512
HALF = 256
QUERY_PIECES = ((0, 64, 44), (64, 64, 44))


def tile_attend_lowertwo_two_postkept_kernel(
    tc, query, cache_words, cache_scales, draft_words, draft_scales, rowf, mix_words, mix_scales,
    offs, offs2, offs3, offs4, offs5, out,
):
    nc = tc.nc
    with ExitStack() as ctx:
        keep = ctx.enter_context(tc.tile_pool(name="keep", bufs=1))
        psum = ctx.enter_context(tc.psum_pool(name="psum", bufs=8))

        def sb(name, shape, dtype, tag=""):
            return keep.tile(shape, dtype, name=name, tag=tag or name, align_bytes=64)

        def load_plane(plane, scales):
            for quad in range(4):
                nc.sync.dma_start(
                    out=plane[32 * quad : 32 * quad + 4, :].bitcast(I32),
                    in_=scales[0, 4 * quad : 4 * quad + 4, :].bitcast(I32),
                )

        cache_plane = sb("cache_plane", [P, T], U8)
        draft_plane = sb("draft_plane", [P, T], U8)
        mix_plane = sb("mix_plane", [P, E], U8)
        for plane in (cache_plane, draft_plane, mix_plane):
            nc.vector.memset(plane[:].bitcast(I32), 0)

        query_rows = query.rearrange("(p j) q -> p j q", j=PACK)
        raw = [sb(f"raw{m0}", [P, PACK, PACK * ms], F32) for m0, ms, share in QUERY_PIECES]
        for c, (m0, ms, share) in enumerate(QUERY_PIECES):
            nc.sync.dma_start(out=raw[c][:], in_=query_rows[:, :, PACK * m0 : PACK * (m0 + ms)])
        load_plane(cache_plane, cache_scales)
        cache_rows = cache_words[0].rearrange("p n t -> p (n t)").bitcast(I32)
        cache_codes = sb("cache_codes", [P, T], I32)
        for h in range(2):
            nc.sync.dma_start(out=cache_codes[:, h * BANK : (h + 1) * BANK], in_=cache_rows[:, h * BANK : (h + 1) * BANK])
        load_plane(draft_plane, draft_scales)
        draft_codes = sb("draft_codes", [P, 2 * T], U8)
        nc.sync.dma_start(out=draft_codes[:].bitcast(I32), in_=draft_words[0].bitcast(I32))
        lists = {}
        for name, src in (("offs", offs), ("offs2", offs2)):
            lists[name] = sb(name, [P, I // 16], U16)
            nc.sync.dma_start(lists[name][:], src)
        row_factor = sb("row_factor", [P, PACK], F32)
        nc.sync.dma_start(out=row_factor[:], in_=rowf.rearrange("(p t) o -> p (t o)", t=PACK))
        mix_codes = sb("mix_codes", [P, 2 * E], U8)
        nc.sync.dma_start(out=mix_codes[:].bitcast(I32), in_=mix_words[0].bitcast(I32))
        load_plane(mix_plane, mix_scales)
        for name, src in (("offs3", offs3), ("offs4", offs4), ("offs5", offs5)):
            lists[name] = sb(name, [P, I // 16], U16)
            nc.sync.dma_start(lists[name][:], src)

        def listed(window, name, first, count):
            return window[:].indirect(lists[name][:, first // 16 : (first + count) // 16])

        pages = [[sb(f"page{et}{k}", [P, Z], F32) for k in range(2)] for et in range(2)]
        for et in range(2):
            for k in range(2):
                nc.vector.memset(pages[et][k][:].bitcast(I32), 0)

        q_bf = sb("q_bf", [P, PACK, P, PACK], BF16)
        for c, (m0, ms, share) in enumerate(QUERY_PIECES):
            src = raw[c][:].rearrange("p j (m t) -> p m t j", t=PACK)
            dst = q_bf[:, :, m0 : m0 + ms, :].rearrange("p t m j -> p m t j")
            nc.scalar.copy(out=dst[:, share:], in_=src[:, share:])
            nc.vector.tensor_copy(out=dst[:, :share], in_=src[:, :share])
        q_codes = [sb(f"q_codes{t}", [P, P], I32) for t in range(PACK)]
        q_plane = [sb(f"q_plane{t}", [P, P], U8) for t in range(PACK)]
        for t in range(PACK):
            nc.vector.quantize_mx(
                out=q_codes[t][:].bitcast(FP8X4), scales=q_plane[t][:],
                in_=q_bf[:, t].rearrange("p m j -> p (m j)"),
            )

        windows = {name: [sb(f"{name}{t}", [P, T], F32) for t in range(PACK)] for name in ("a", "b")}
        low = sb("low", [P, PACK, HALF], F32)

        def scores(name, t):
            for h in range(2):
                cols = slice(h * BANK, (h + 1) * BANK)
                bank = psum.tile([P, BANK], F32, name="bank")
                if name == "a":
                    rhs, rhs_scale = cache_codes[:, cols].bitcast(FP8X4), cache_plane[:, cols]
                else:
                    rhs, rhs_scale = draft_codes[:, 2 * h * BANK : 2 * (h + 1) * BANK].bitcast(FP4X4), draft_plane[:, cols]
                nc.tensor.matmul_mx(
                    out=bank[:], lhsT=q_codes[t][:].bitcast(FP8X4), lhsT_scale=q_plane[t][:],
                    rhs=rhs, rhs_scale=rhs_scale, start=True, stop=True,
                )
                if h == 0:
                    nc.scalar.copy(out=windows[name][t][:, cols], in_=bank[:])
                else:
                    nc.vector.tensor_copy(out=windows[name][t][:, cols], in_=bank[:])

        def gather(dst, name, t, h, on_scalar):
            src = listed(windows[name][t], "offs" if name == "a" else "offs2", h * HALF, HALF)
            if on_scalar:
                nc.scalar.activation(dst, src, COPY)
            else:
                nc.vector.tensor_copy(dst, src)

        def take_lower(x, y, dst=None):
            nc.vector.tensor_tensor(x if dst is None else dst, x, y, MIN)

        o1 = sb("o1", [P, 2, I], F32)

        def weigh(rounded, g, ts):
            for t in ts:
                nc.vector.tensor_scalar(rounded[:, t, :], g[:, t, :], row_factor[:, t : t + 1], None, MULT)

        def mix(rounded, first, apart, tag=""):
            gw = sb(f"gw{first}", [P, 128, PACK], BF16, tag=tag)
            nc.vector.tensor_copy(
                out=gw[:].rearrange("p (c i) t -> p c t i", i=4), in_=rounded[:].rearrange("p t (c i) -> p c t i", i=4)
            )
            codes = sb(f"gw_codes{first}", [P, 128], I32)
            plane = sb(f"gw_plane{first}", [P, 128], U8)
            nc.vector.quantize_mx(out=codes[:].bitcast(FP8X4), scales=plane[:], in_=gw[:].rearrange("p i t -> p (i t)"))
            for et in range(2):
                bank = psum.tile([P, BANK], F32, name="bank")
                nc.tensor.matmul_mx(
                    out=bank[:, :128], lhsT=mix_codes[:, 2 * P * et : 2 * P * (et + 1)].bitcast(FP4X4),
                    lhsT_scale=mix_plane[:, P * et : P * (et + 1)],
                    rhs=codes[:].bitcast(FP8X4), rhs_scale=plane[:], start=True, stop=True,
                )
                if apart:
                    nc.scalar.copy(out=o1[:, et, first : first + 128], in_=bank[:, :128])
                else:
                    nc.vector.tensor_copy(out=o1[:, et, first : first + 128], in_=bank[:, :128])

        def scatter(et, first, count):
            for k, name in enumerate(("offs3", "offs4")):
                nc.scalar.activation(listed(pages[et][k], name, first, count), o1[:, et, first : first + count], COPY)

        def lower_page(et):
            m1 = sb(f"m1_{et}", [P, Z], F32, tag="m1")
            nc.vector.tensor_tensor(m1[:], pages[et][0][:], pages[et][1][:], MIN)
            return m1

        rounded = [sb(f"rounded{c}", [P, PACK, 128], BF16) for c in range(3)]
        scores("a", 0)
        gather(low[:, 0, :], "a", 0, 0, False)
        for name, t in (("a", 1), ("b", 0), ("b", 1), ("a", 2), ("b", 2), ("a", 3), ("b", 3)):
            scores(name, t)
        other = sb("other", [P, PACK, HALF], F32, tag="cache_codes")
        gather(low[:, 1, :], "a", 1, 0, True)
        gather(other[:, 0, :], "b", 0, 0, False)
        gather(other[:, 1, :], "b", 1, 0, True)
        gather(other[:, 2, :], "b", 2, 0, False)
        gather(low[:, 2, :], "a", 2, 0, True)
        gather(other[:, 3, :], "b", 3, 0, False)
        gather(low[:, 3, :], "a", 3, 0, True)
        take_lower(low[:, :2, :128], other[:, :2, :128])
        take_lower(low[:, 2:, :128], other[:, 2:, :128])
        weigh(rounded[0], low[:, :, :128], range(PACK))
        late = sb("late", [P, PACK, HALF], F32, tag="draft_codes")
        for t in range(PACK):
            gather(late[:, t, :], "a", t, 1, True)
        mix(rounded[0], 0, True)
        for et in range(2):
            scatter(et, 0, 128)
        g1 = sb("g1", [P, PACK, 128], F32, tag="gw0")
        take_lower(low[:, :, 128:], other[:, :, 128:], g1[:])
        weigh(rounded[1], g1[:], range(PACK))
        mix(rounded[1], 128, False)
        for et in range(2):
            scatter(et, 128, 128)
        third = sb("third", [P, HALF], F32, tag="gw128")
        fourth = sb("fourth", [P, HALF], F32, tag="gw_codes128")
        for t, dst in enumerate((low[:, 0, :], low[:, 1, :], third[:], fourth[:])):
            gather(dst, "b", t, 1, False)
        for c in (2, 3):
            cols = slice(128 * (c - 2), 128 * (c - 1))
            take_lower(late[:, :2, cols], low[:, :2, cols])
            take_lower(late[:, 2, cols], third[:, cols])
            take_lower(late[:, 3, cols], fourth[:, cols])
            if c == 3:
                rounded.append(sb("rounded3", [P, PACK, 128], BF16, tag="gw256"))
            weigh(rounded[c], late[:, :, cols], range(PACK))
            mix(rounded[c], 128 * c, False)
        scatter(0, 256, 128)
        scatter(0, 384, 128)
        m1 = lower_page(0)
        y0 = sb("y0", [P, I], F32)
        nc.vector.tensor_tensor(y0[:], listed(m1, "offs5", 0, I), o1[:, 0, :], ADD)
        nc.sync.dma_start(out=out[:P, :], in_=y0[:])
        scatter(1, 256, 256)
        m1 = lower_page(1)
        y1 = [sb(f"y1{h}", [P, HALF], F32) for h in range(2)]
        kept = sb("kept", [P, HALF], F32)
        nc.scalar.activation(kept[:], listed(m1, "offs5", HALF, HALF), COPY)
        nc.vector.tensor_tensor(y1[0][:], listed(m1, "offs5", 0, HALF), o1[:, 1, :HALF], ADD)
        nc.sync.dma_start(out=out[P:, :HALF], in_=y1[0][:])
        nc.vector.tensor_tensor(y1[1][:], kept[:], o1[:, 1, HALF:], ADD)
        nc.sync.dma_start(out=out[P:, HALF:], in_=y1[1][:])
